import numpy as np
import ml_dtypes


def mxq(x, axis, fmt="e4m3"):
    dtype, down = {"e4m3": (ml_dtypes.float8_e4m3fn, 7), "e5m2": (ml_dtypes.float8_e5m2, 14)}[fmt]
    v = np.moveaxis(np.asarray(x, np.float32).astype(ml_dtypes.bfloat16).astype(np.float64), axis, -1)
    blocks = v.reshape(v.shape[:-1] + (-1, 32))
    amax = np.abs(blocks).max(-1, keepdims=True)
    byte = np.maximum(np.where(amax > 0, np.frexp(amax)[1] - 1 + 127, 0) - down, 1)
    scale = np.exp2(byte - 127.0)
    codes = (blocks / scale).astype(np.float32).astype(dtype).astype(np.float64)
    return np.moveaxis((codes * scale).reshape(v.shape), -1, axis)


WIDE = False


def mx_kscale(k):
    if not WIDE:
        return np.ones(k)
    levels = np.array([10, -10, 5, -5, 0])
    if k % 512:
        return np.exp2(np.random.permutation(np.resize(levels, k // 32))).repeat(32)
    a = np.empty((k // 512, 16))
    for p in range(k // 512):
        a[p, :8] = np.random.permutation(np.resize(levels, 8))
        for g in range(8):
            far = levels[np.abs(levels - a[p, g]) >= 10]
            a[p, g + 8] = far[np.random.randint(len(far))]
    return np.exp2(a.ravel()).repeat(32)


BF16 = ml_dtypes.bfloat16


def bf(x):
    return np.asarray(x, np.float32).astype(BF16)


def f64(x):
    return np.asarray(x).astype(np.float64)


E2M1 = np.array([0.0, 0.5, 1.0, 1.5, 2.0, 3.0, 4.0, 6.0, -0.0, -0.5, -1.0, -1.5, -2.0, -3.0, -4.0, -6.0])


def pack_weight(w, fmt):
    k, n = w.shape
    w = f64(bf(w)).reshape(k // 32, 32, n)
    amax = np.abs(w).max(1)
    if fmt == "e4m3":
        byte = np.frexp(amax)[1] - 1 + 127 - 7
    else:
        mant, ex = np.frexp(amax / 6.0)
        byte = np.where(mant > 0.5, ex, ex - 1) + 127
    byte = np.clip(np.where(amax > 0, byte, 1), 1, 254)
    scaled = (w * np.exp2(127.0 - byte)[:, None, :]).reshape(k, n).astype(np.float32)
    by_word = np.ascontiguousarray(scaled.reshape(k // 512, 128, 4, n).transpose(0, 1, 3, 2))
    if fmt == "e4m3":
        words = by_word.astype(ml_dtypes.float8_e4m3fn).view(np.uint8)
    else:
        c = by_word.astype(ml_dtypes.float4_e2m1fn).view(np.uint8) & 0xF
        words = c[..., 0::2] | (c[..., 1::2] << 4)
    return np.ascontiguousarray(words), np.ascontiguousarray(byte.astype(np.uint8).reshape(k // 512, 16, n))


def unpack_weight(words, scales, fmt):
    g, p, n, _ = words.shape
    if fmt == "e4m3":
        vals = np.ascontiguousarray(words).view(ml_dtypes.float8_e4m3fn).astype(np.float64)
    else:
        nib = np.empty((g, p, n, 4), np.uint8)
        nib[..., 0::2] = words & 0xF
        nib[..., 1::2] = words >> 4
        vals = E2M1[nib]
    vals = vals * np.repeat(np.exp2(scales.astype(np.float64) - 127.0), 8, axis=1)[..., None]
    return vals.transpose(0, 1, 3, 2).reshape(g * 512, n)
def pack4(w):
    words, scales = pack_weight(w, "e2m1")
    return words.reshape(words.shape[0], 128, -1), scales


def unpack4(words, scales):
    return unpack_weight(words.reshape(words.shape[0], 128, -1, 2), scales, "e2m1")


E, S, L, T = 4, 512, 1024, 1024


def draw0():
    s = mx_kscale(S)
    t = mx_kscale(L)
    trans = np.random.standard_normal((E, S, L)) / np.sqrt(S) / s[:, None] * t
    pol = np.random.standard_normal((E, L, S)) / np.sqrt(L) / t[:, None]
    trans_words, trans_scales = pack4(trans.reshape(E * S, L))
    pol_words, pol_scales = pack4(pol.reshape(E * L, S))
    return {"values": bf(np.random.standard_normal((E, S, T)) * s[:, None]),
            "trans_words": trans_words,
            "trans_scales": trans_scales,
            "gamma": bf(np.random.uniform(0.5, 0.95, (E, T))),
            "reward": bf(0.5 * np.random.standard_normal((E, L, T)) * t[:, None]),
            "pol_words": pol_words,
            "pol_scales": pol_scales}


def core(values, trans_words, trans_scales, gamma, reward, pol_words, pol_scales):
    a = unpack4(trans_words, trans_scales).reshape(E, S, L)
    b = unpack4(pol_words, pol_scales).reshape(E, L, S)
    nxt = a.swapaxes(1, 2) @ mxq(f64(values), 1, "e4m3")
    backed = f64(reward) + f64(gamma)[:, None, :] * nxt
    return b.swapaxes(1, 2) @ mxq(backed, 1, "e4m3")


def e4m3fn_bytes(y):
    return np.clip(np.asarray(y, np.float64), -448.0, 448.0).astype(np.float32).astype(ml_dtypes.float8_e4m3fn).view(np.uint8)


def e4m3fn_values(b):
    return np.asarray(b, np.uint8).view(ml_dtypes.float8_e4m3fn).astype(np.float64)


def setup_inputs():
    d = draw0()
    x0 = np.asarray(d['values']).astype(np.float64)
    s = (np.max(np.abs(x0), axis=(0, 2), keepdims=True) / 448.0).astype(np.float32)
    out = {}
    for k, v in d.items():
        if k == 'values':
            out['values_bytes'] = e4m3fn_bytes(x0 / s.astype(np.float64))
            out['values_scale'] = s
        else:
            out[k] = v
    return out


def reference(values_bytes, values_scale, trans_words, trans_scales, gamma, reward, pol_words, pol_scales):
    return core(e4m3fn_values(values_bytes) * values_scale.astype(np.float64), trans_words, trans_scales, gamma, reward, pol_words, pol_scales)

@@ -1,0 +1,344 @@
+from contextlib import ExitStack
+
+import concourse.mybir as mybir
+from concourse.masks import make_identity
+
+E, S, L, T = 4, 512, 1024, 1024
+
+FLOPS = 2 * E * (L * S * T + S * L * T)
+
+F32 = mybir.dt.float32
+BF16 = mybir.dt.bfloat16
+I32 = mybir.dt.int32
+U32 = mybir.dt.uint32
+U8 = mybir.dt.uint8
+FP8 = mybir.dt.float8_e4m3fn
+FP8X4 = mybir.dt.float8_e4m3fn_x4
+FP4X4 = mybir.dt.float4_e2m1fn_x4
+COPY = mybir.ActivationFunctionType.Copy
+MULT = mybir.AluOpType.mult
+ADD = mybir.AluOpType.add
+
+P = 128
+PACK = 4
+HALF = 512
+QUARTER = 256
+G = L // 512
+STEPS = 32
+V_PLANES = (0,)
+RUN = 4
+
+
+def tile_multi_world_bellman_backup_s14_kernel(
+    tc, values_bytes, values_scale, trans_words, trans_scales, gamma, reward, pol_words, pol_scales, out
+):
+    nc = tc.nc
+    with ExitStack() as ctx:
+        keep = ctx.enter_context(tc.tile_pool(name="keep", bufs=1))
+        work = ctx.enter_context(tc.tile_pool(name="work", bufs=2))
+        psum = ctx.enter_context(tc.psum_pool(name="psum", bufs=2))
+        ctx.enter_context(tc.manual_schedule())
+
+        vscale = keep.tile([P, PACK], F32, name="vscale")
+        nc.sync.dma_start(out=vscale[:], in_=values_scale.rearrange("o (p t) u -> p (o t u)", t=PACK))
+
+        vbytes = {}
+
+        def load_values(e, lo, hi):
+            vb = keep.tile([P, PACK, hi - lo], U8, name="vb_%d_%d" % (e, lo))
+            src = values_bytes[e].rearrange("(p t) n -> p t n", t=PACK)
+            nc.sync.dma_start(out=vb[:], in_=src[:, :, lo:hi])
+            vbytes[(e, lo, hi)] = vb
+
+        def values_view(e, t, lo, hi):
+            for key, vb in vbytes.items():
+                if key[0] == e and key[1] <= lo and hi <= key[2]:
+                    return vb[:, t, lo - key[1] : hi - key[1]].bitcast(FP8)
+            raise AssertionError("no tile of values")
+
+        tw = []
+
+        def load_trans(e):
+            w = keep.tile([P, 2 * L], U8, name="tw_%d" % e, align_bytes=64)
+            nc.sync.dma_start(out=w[:], in_=trans_words[e])
+            tw.append(w)
+
+        pw = []
+
+        def load_pol(e):
+            w = keep.tile([P, G, 2 * S], U8, name="pw_%d" % e, align_bytes=64)
+            nc.sync.dma_start(out=w[:], in_=pol_words[G * e : G * e + G].rearrange("g p n -> p g n"))
+            pw.append(w)
+
+        rew = {}
+
+        def load_reward(e, g, lo, hi):
+            r = keep.tile([P, PACK, hi - lo], BF16, name="rew_%d_%d_%d" % (e, g, lo))
+            src = reward[e].rearrange("(g p t) n -> g p t n", p=P, t=PACK)[g]
+            nc.sync.dma_start(out=r[:], in_=src[:, :, lo:hi])
+            rew[(e, g, lo, hi)] = r
+
+        def reward_view(e, g, lo, hi):
+            for key, r in rew.items():
+                if key[0] == e and key[1] == g and key[2] <= lo and hi <= key[3]:
+                    return r[:, :, lo - key[2] : hi - key[2]]
+            raise AssertionError("no tile of reward")
+
+        ident = keep.tile([P, P], F32, name="ident")
+        tsc = keep.tile([P, E, L], U8, name="tsc", align_bytes=64)
+        psc = keep.tile([P, E * G, S], U8, name="psc", align_bytes=64)
+        gam_rows = keep.tile([P, P], BF16, name="gam_rows")
+        gam_f32 = keep.tile([P, P], F32, name="gam_f32")
+        gcol = keep.tile([P, 32], F32, name="gcol")
+        nc.vector.memset(tsc[:].rearrange("p e n -> p (e n)").bitcast(I32), 0)
+        nc.gpsimd.memset(gam_rows[:], 0.0)
+        make_identity(nc, ident[:])
+        nc.vector.memset(psc[:].rearrange("p e n -> p (e n)").bitcast(I32), 0)
+
+        load_values(0, 0, QUARTER)
+        nc.sync.dma_start(out=gam_rows[0:32, :], in_=gamma.rearrange("e (j p) -> (e j) p", p=P))
+        load_trans(0)
+        for q in range(4):
+            nc.sync.dma_start(
+                out=tsc[32 * q : 32 * q + 4].bitcast(I32),
+                in_=trans_scales[:, 4 * q : 4 * q + 4, :].rearrange("g q n -> q g n").bitcast(I32),
+            )
+        load_reward(0, 0, 0, HALF)
+        load_values(0, QUARTER, HALF)
+        load_values(0, HALF, T)
+        load_reward(0, 1, 0, HALF)
+        for q in range(4):
+            nc.sync.dma_start(
+                out=psc[32 * q : 32 * q + 4].bitcast(I32),
+                in_=pol_scales[:, 4 * q : 4 * q + 4, :].rearrange("g q n -> q g n").bitcast(I32),
+            )
+        load_pol(0)
+        load_reward(0, 0, HALF, T)
+        load_reward(0, 1, HALF, T)
+
+        def load_world(e):
+            load_values(e, 0, T)
+            load_trans(e)
+            load_reward(e, 0, 0, T)
+            load_reward(e, 1, 0, T)
+            load_pol(e)
+
+        load_world(1)
+
+        wide = {}
+
+        def widen(s, t, on_vector, lo=0, hi=HALF):
+            e, h = divmod(s, 2)
+            if s not in wide:
+                w = work.tile([P, PACK, HALF], BF16, name="wide", align_bytes=64)
+                wide[s] = w
+            src = values_view(e, t, HALF * h + lo, HALF * h + hi)
+            dst = wide[s][:, t, lo:hi]
+            if on_vector:
+                nc.vector.tensor_scalar(out=dst, in0=src, scalar1=vscale[:, t : t + 1], scalar2=None, op0=MULT)
+            else:
+                nc.scalar.activation(out=dst, in_=src, func=COPY, scale=vscale[:, t : t + 1])
+
+        inter = {}
+
+        def interleave(p, half):
+            s, jp = divmod(p, 2)
+            if half == 0:
+                x = work.tile([P, QUARTER, PACK], BF16, name="inter", align_bytes=64, bufs=3)
+                inter[p] = x
+            cols = slice(128 * half, 128 * half + 128)
+            src = wide[s][:, :, QUARTER * jp + 128 * half : QUARTER * jp + 128 * half + 128]
+            nc.vector.tensor_copy(
+                out=inter[p][:, cols, :].rearrange("p (c i) t -> p c t i", i=RUN),
+                in_=src.rearrange("p t (c i) -> p c t i", i=RUN),
+            )
+
+        vcodes = {}
+
+        def quant_v(p):
+            c = work.tile([P, QUARTER], U32, name="vcodes", align_bytes=64, bufs=3)
+            sc = work.tile([P, QUARTER], U8, name="vcodes_sc", align_bytes=64, bufs=3)
+            nc.vector.quantize_mx(
+                out=c[:].bitcast(FP8X4), scales=sc[:], in_=inter[p][:].rearrange("p n t -> p (n t)")
+            )
+            vcodes[p] = (c, sc)
+
+        nxt = {}
+
+        def first_matmul(k):
+            p, g = divmod(k, 2)
+            e = k // 8
+            c, sc = vcodes[p]
+            for j in range(2):
+                b = psum.tile([P, 512], F32, name="nxt", bufs=3)
+                cols = slice(128 * j, 128 * j + 128)
+                nc.tensor.matmul_mx(
+                    out=b[:],
+                    lhsT=c[:, cols].bitcast(FP8X4),
+                    lhsT_scale=sc[:, cols],
+                    rhs=tw[e][:, 1024 * g : 1024 * g + 1024].bitcast(FP4X4),
+                    rhs_scale=tsc[:, e, 512 * g : 512 * g + 512],
+                    start=True,
+                    stop=True,
+                )
+                nxt[(k, j)] = b
+
+        disc = {}
+
+        def discount(k):
+            p = k // 2
+            for j in range(2):
+                jt = 2 * p + j
+                d = work.tile([P, PACK, P], F32, name="disc", bufs=5)
+                nc.scalar.activation(
+                    out=d[:],
+                    in_=nxt[(k, j)][:].rearrange("p (m t) -> p t m", t=PACK),
+                    func=COPY,
+                    scale=gcol[:, jt : jt + 1],
+                )
+                disc[(k, j)] = d
+
+        turned = {}
+
+        def transposes(k):
+            for j in range(2):
+                b = psum.tile([P, PACK, P], F32, name="turned", bufs=3)
+                for t in range(PACK):
+                    nc.tensor.transpose(b[:, t, :], disc[(k, j)][:, t, :], ident[:])
+                turned[(k, j)] = b
+
+        backed = {}
+
+        def add_reward(k, j):
+            p, g = divmod(k, 2)
+            e, jt0 = p // 4, 2 * (p % 4)
+            if j == 0:
+                q = work.tile([P, QUARTER, PACK], BF16, name="backed", align_bytes=64, bufs=3)
+                backed[k] = q
+            lo = 128 * (jt0 + j)
+            nc.vector.tensor_tensor(
+                out=backed[k][:, 128 * j : 128 * j + 128, :].rearrange("p (c i) t -> p c t i", i=RUN),
+                in0=turned[(k, j)][:].rearrange("p t (c i) -> p c t i", i=RUN),
+                in1=reward_view(e, g, lo, lo + 128).rearrange("p t (c i) -> p c t i", i=RUN),
+                op=ADD,
+            )
+
+        qcodes = {}
+
+        def quant_q(k):
+            p, g = divmod(k, 2)
+            s, jp = divmod(p, 2)
+            if jp == 0:
+                c = work.tile([P, HALF], U32, name="qcodes_%d" % g, align_bytes=64)
+                sc = work.tile([P, HALF], U8, name="qcodes_sc_%d" % g, align_bytes=64)
+                qcodes[(s, g)] = (c, sc)
+            c, sc = qcodes[(s, g)]
+            cols = slice(QUARTER * jp, QUARTER * jp + QUARTER)
+            nc.vector.quantize_mx(
+                out=c[:, cols].bitcast(FP8X4), scales=sc[:, cols], in_=backed[k][:].rearrange("p n t -> p (n t)")
+            )
+
+        accs = {}
+
+        def second_matmul(s, m, lo, hi, tag, bufs):
+            e = s // 2
+            b = psum.tile([P, hi - lo], F32, name=tag, bufs=bufs)
+            n = HALF if hi - lo == HALF else P
+            for a in range(lo, hi, n):
+                for g in range(G):
+                    c, sc = qcodes[(s, g)]
+                    nc.tensor.matmul_mx(
+                        out=b[:, a - lo : a - lo + n],
+                        lhsT=pw[e][:, g, 256 * m : 256 * m + 256].bitcast(FP4X4),
+                        lhsT_scale=psc[:, G * e + g, 128 * m : 128 * m + 128],
+                        rhs=c[:, a : a + n].bitcast(FP8X4),
+                        rhs_scale=sc[:, a : a + n],
+                        start=(g == 0),
+                        stop=(g == G - 1),
+                    )
+            accs[(s, m, lo)] = b
+
+        res = {}
+
+        def empty(s, m, lo, hi, on_vector):
+            if lo == 0:
+                r = work.tile([P, HALF], F32, name="res", bufs=8)
+                res[(s, m)] = r
+            r = res[(s, m)]
+            if on_vector:
+                nc.vector.tensor_copy(out=r[:, lo:hi], in_=accs[(s, m, lo)][:])
+            else:
+                nc.scalar.copy(out=r[:, lo:hi], in_=accs[(s, m, lo)][:])
+            if hi == HALF:
+                e, h = divmod(s, 2)
+                nc.sync.dma_start(out=out[e, 128 * m : 128 * m + 128, HALF * h : HALF * h + HALF], in_=r[:])
+
+        widen_at, inter_at, quant_at, out_at = {}, {}, {}, {}
+        for s in range(1, 8):
+            on_s = [t for t in range(PACK) if t not in V_PLANES]
+            for i, t in enumerate(on_s):
+                widen_at.setdefault(max(4 * s - 8 + i, 0), []).append((s, t, False))
+            for t in V_PLANES:
+                widen_at.setdefault(max(4 * s - 7, 0), []).append((s, t, True))
+        for p in range(2, 16):
+            inter_at.setdefault(max(2 * p - 5, 0), []).append((p, 0))
+            inter_at.setdefault(2 * p - 4, []).append((p, 1))
+            quant_at.setdefault(2 * p - 3, []).append(p)
+        for s in range(7):
+            for m in range(4):
+                out_at.setdefault(min(4 * s + 5 + m, STEPS - 1), []).append((s, m))
+
+        for t in (0, 1):
+            widen(0, t, False, 0, QUARTER)
+            widen(0, t + 2, True, 0, QUARTER)
+        nc.vector.tensor_copy(out=gam_f32[:], in_=gam_rows[:])
+        interleave(0, 0)
+        interleave(0, 1)
+        quant_v(0)
+        turned_gamma = psum.tile([P, P], F32, name="acc", bufs=2)
+        nc.tensor.transpose(turned_gamma[:], gam_f32[:], ident[:])
+        nc.scalar.copy(out=gcol[:], in_=turned_gamma[:, 0:32])
+        first_matmul(0)
+        discount(0)
+        for t in (0, 1):
+            widen(0, t, False, QUARTER, HALF)
+            widen(0, t + 2, True, QUARTER, HALF)
+        interleave(1, 0)
+        interleave(1, 1)
+
+        for k in range(STEPS):
+            if k == 4:
+                load_world(2)
+            if k == 12:
+                load_world(3)
+            if k == 0:
+                quant_v(1)
+            if k + 1 < STEPS:
+                first_matmul(k + 1)
+                discount(k + 1)
+            for s, m in out_at.get(k, []):
+                second_matmul(s, m, 0, HALF, "acc", 2)
+            transposes(k)
+            for s, m in out_at.get(k, []):
+                empty(s, m, 0, HALF, False)
+            add_reward(k, 0)
+            if k >= 1:
+                quant_q(k - 1)
+            for p in quant_at.get(k, []):
+                quant_v(p)
+            add_reward(k, 1)
+            for s, t, on_vector in widen_at.get(k, []):
+                widen(s, t, on_vector)
+            for p, half in inter_at.get(k, []):
+                interleave(p, half)
+
+        tags = [("acc", 2), ("acc", 2), ("nxt", 3), ("nxt", 3)]
+        for m in range(4):
+            second_matmul(7, m, 0, QUARTER, tags[m][0], tags[m][1])
+            empty(7, m, 0, QUARTER, m % 2 == 1)
+        quant_q(STEPS - 1)
+        tags = [("nxt", 3), ("turned", 3), ("turned", 3), ("turned", 3)]
+        for m in range(4):
+            second_matmul(7, m, QUARTER, HALF, tags[m][0], tags[m][1])
+        for m in range(4):
+            empty(7, m, QUARTER, HALF, m % 2 == 1)

@@ -97,16 +97,19 @@ def tile_multi_world_bellman_backup_s14_kernel(
 
         load_values(0, 0, QUARTER)
         nc.sync.dma_start(out=gam_rows[0:32, :], in_=gamma.rearrange("e (j p) -> (e j) p", p=P))
-        load_trans(0)
         for q in range(4):
             nc.sync.dma_start(
                 out=tsc[32 * q : 32 * q + 4].bitcast(I32),
                 in_=trans_scales[:, 4 * q : 4 * q + 4, :].rearrange("g q n -> q g n").bitcast(I32),
             )
-        load_reward(0, 0, 0, HALF)
+        load_trans(0)
+        load_reward(0, 0, 0, QUARTER)
+        load_reward(0, 1, 0, QUARTER)
         load_values(0, QUARTER, HALF)
         load_values(0, HALF, T)
-        load_reward(0, 1, 0, HALF)
+        load_values(1, 0, T)
+        load_reward(0, 0, QUARTER, HALF)
+        load_reward(0, 1, QUARTER, HALF)
         for q in range(4):
             nc.sync.dma_start(
                 out=psc[32 * q : 32 * q + 4].bitcast(I32),
@@ -117,7 +120,8 @@ def tile_multi_world_bellman_backup_s14_kernel(
         load_reward(0, 1, HALF, T)
 
         def load_world(e):
-            load_values(e, 0, T)
+            if e > 1:
+                load_values(e, 0, T)
             load_trans(e)
             load_reward(e, 0, 0, T)
             load_reward(e, 1, 0, T)
@@ -141,37 +145,35 @@ def tile_multi_world_bellman_backup_s14_kernel(
 
         inter = {}
 
-        def interleave(p, half):
-            s, jp = divmod(p, 2)
-            if half == 0:
-                x = work.tile([P, QUARTER, PACK], BF16, name="inter", align_bytes=64, bufs=3)
-                inter[p] = x
-            cols = slice(128 * half, 128 * half + 128)
-            src = wide[s][:, :, QUARTER * jp + 128 * half : QUARTER * jp + 128 * half + 128]
+        def interleave(s, lo, hi):
+            x = work.tile([P, hi - lo, PACK], BF16, name="inter", align_bytes=64)
+            inter[(s, lo)] = x
+            src = wide[s][:, :, lo:hi]
             nc.vector.tensor_copy(
-                out=inter[p][:, cols, :].rearrange("p (c i) t -> p c t i", i=RUN),
+                out=x[:].rearrange("p (c i) t -> p c t i", i=RUN),
                 in_=src.rearrange("p t (c i) -> p c t i", i=RUN),
             )
 
         vcodes = {}
 
-        def quant_v(p):
-            c = work.tile([P, QUARTER], U32, name="vcodes", align_bytes=64, bufs=3)
-            sc = work.tile([P, QUARTER], U8, name="vcodes_sc", align_bytes=64, bufs=3)
+        def quant_v(s, lo, hi):
+            c = work.tile([P, hi - lo], U32, name="vcodes", align_bytes=64, bufs=3)
+            sc = work.tile([P, hi - lo], U8, name="vcodes_sc", align_bytes=64, bufs=3)
             nc.vector.quantize_mx(
-                out=c[:].bitcast(FP8X4), scales=sc[:], in_=inter[p][:].rearrange("p n t -> p (n t)")
+                out=c[:].bitcast(FP8X4), scales=sc[:], in_=inter[(s, lo)][:].rearrange("p n t -> p (n t)")
             )
-            vcodes[p] = (c, sc)
+            for a in range(lo, hi, QUARTER):
+                vcodes[2 * s + a // QUARTER] = (c, sc, a - lo)
 
         nxt = {}
 
         def first_matmul(k):
             p, g = divmod(k, 2)
             e = k // 8
-            c, sc = vcodes[p]
+            c, sc, base = vcodes[p]
             for j in range(2):
                 b = psum.tile([P, 512], F32, name="nxt", bufs=3)
-                cols = slice(128 * j, 128 * j + 128)
+                cols = slice(base + 128 * j, base + 128 * j + 128)
                 nc.tensor.matmul_mx(
                     out=b[:],
                     lhsT=c[:, cols].bitcast(FP8X4),
@@ -189,7 +191,7 @@ def tile_multi_world_bellman_backup_s14_kernel(
             p = k // 2
             for j in range(2):
                 jt = 2 * p + j
-                d = work.tile([P, PACK, P], F32, name="disc", bufs=5)
+                d = work.tile([P, PACK, P], F32, name="disc", bufs=6)
                 nc.scalar.activation(
                     out=d[:],
                     in_=nxt[(k, j)][:].rearrange("p (m t) -> p t m", t=PACK),
@@ -212,12 +214,14 @@ def tile_multi_world_bellman_backup_s14_kernel(
         def add_reward(k, j):
             p, g = divmod(k, 2)
             e, jt0 = p // 4, 2 * (p % 4)
-            if j == 0:
-                q = work.tile([P, QUARTER, PACK], BF16, name="backed", align_bytes=64, bufs=3)
-                backed[k] = q
+            s, jp = divmod(p, 2)
+            if j == 0 and jp == 0:
+                q = work.tile([P, HALF, PACK], BF16, name="backed_%d" % g, align_bytes=64, bufs=2)
+                backed[(s, g)] = q
             lo = 128 * (jt0 + j)
+            at = QUARTER * jp + 128 * j
             nc.vector.tensor_tensor(
-                out=backed[k][:, 128 * j : 128 * j + 128, :].rearrange("p (c i) t -> p c t i", i=RUN),
+                out=backed[(s, g)][:, at : at + 128, :].rearrange("p (c i) t -> p c t i", i=RUN),
                 in0=turned[(k, j)][:].rearrange("p t (c i) -> p c t i", i=RUN),
                 in1=reward_view(e, g, lo, lo + 128).rearrange("p t (c i) -> p c t i", i=RUN),
                 op=ADD,
@@ -225,17 +229,16 @@ def tile_multi_world_bellman_backup_s14_kernel(
 
         qcodes = {}
 
-        def quant_q(k):
-            p, g = divmod(k, 2)
-            s, jp = divmod(p, 2)
-            if jp == 0:
+        def quant_q(s, g, lo, hi):
+            if lo == 0:
                 c = work.tile([P, HALF], U32, name="qcodes_%d" % g, align_bytes=64)
                 sc = work.tile([P, HALF], U8, name="qcodes_sc_%d" % g, align_bytes=64)
                 qcodes[(s, g)] = (c, sc)
             c, sc = qcodes[(s, g)]
-            cols = slice(QUARTER * jp, QUARTER * jp + QUARTER)
             nc.vector.quantize_mx(
-                out=c[:, cols].bitcast(FP8X4), scales=sc[:, cols], in_=backed[k][:].rearrange("p n t -> p (n t)")
+                out=c[:, lo:hi].bitcast(FP8X4),
+                scales=sc[:, lo:hi],
+                in_=backed[(s, g)][:, lo:hi, :].rearrange("p n t -> p (n t)"),
             )
 
         accs = {}
@@ -273,17 +276,23 @@ def tile_multi_world_bellman_backup_s14_kernel(
                 e, h = divmod(s, 2)
                 nc.sync.dma_start(out=out[e, 128 * m : 128 * m + 128, HALF * h : HALF * h + HALF], in_=r[:])
 
-        widen_at, inter_at, quant_at, out_at = {}, {}, {}, {}
-        for s in range(1, 8):
+        widen_at, inter_at, quant_at, quant_q_at, out_at = {}, {}, {}, {}, {}
+        for s in range(2, 8):
             on_s = [t for t in range(PACK) if t not in V_PLANES]
             for i, t in enumerate(on_s):
-                widen_at.setdefault(max(4 * s - 8 + i, 0), []).append((s, t, False))
+                widen_at.setdefault(4 * s - 7 + i, []).append((s, t, False))
             for t in V_PLANES:
-                widen_at.setdefault(max(4 * s - 7, 0), []).append((s, t, True))
-        for p in range(2, 16):
-            inter_at.setdefault(max(2 * p - 5, 0), []).append((p, 0))
-            inter_at.setdefault(2 * p - 4, []).append((p, 1))
-            quant_at.setdefault(2 * p - 3, []).append(p)
+                widen_at.setdefault(4 * s - 6, []).append((s, t, True))
+        widen_at[0] = [(1, 2, False), (1, 3, False)]
+        for s in range(1, 8):
+            inter_at.setdefault(max(4 * s - 4, 1), []).append(s)
+            quant_at.setdefault(max(4 * s - 3, 2), []).append(s)
+        for s in range(7):
+            for g in range(G):
+                quant_q_at.setdefault(4 * s + 3 + g, []).append((s, g, 0, HALF))
+        for k in range(28, STEPS - 1):
+            lo = QUARTER * ((k - 28) // 2)
+            quant_q_at.setdefault(k + 1, []).append((7, k % 2, lo, lo + QUARTER))
         for s in range(7):
             for m in range(4):
                 out_at.setdefault(min(4 * s + 5 + m, STEPS - 1), []).append((s, m))
@@ -292,27 +301,25 @@ def tile_multi_world_bellman_backup_s14_kernel(
             widen(0, t, False, 0, QUARTER)
             widen(0, t + 2, True, 0, QUARTER)
         nc.vector.tensor_copy(out=gam_f32[:], in_=gam_rows[:])
-        interleave(0, 0)
-        interleave(0, 1)
-        quant_v(0)
+        interleave(0, 0, QUARTER)
+        quant_v(0, 0, QUARTER)
         turned_gamma = psum.tile([P, P], F32, name="acc", bufs=2)
         nc.tensor.transpose(turned_gamma[:], gam_f32[:], ident[:])
         nc.scalar.copy(out=gcol[:], in_=turned_gamma[:, 0:32])
         first_matmul(0)
         discount(0)
-        for t in (0, 1):
-            widen(0, t, False, QUARTER, HALF)
-            widen(0, t + 2, True, QUARTER, HALF)
-        interleave(1, 0)
-        interleave(1, 1)
+        for t in range(PACK):
+            widen(0, t, True, QUARTER, HALF)
+        interleave(0, QUARTER, HALF)
+        widen(1, 0, True)
+        quant_v(0, QUARTER, HALF)
+        widen(1, 1, True)
 
         for k in range(STEPS):
             if k == 4:
                 load_world(2)
             if k == 12:
                 load_world(3)
-            if k == 0:
-                quant_v(1)
             if k + 1 < STEPS:
                 first_matmul(k + 1)
                 discount(k + 1)
@@ -322,21 +329,21 @@ def tile_multi_world_bellman_backup_s14_kernel(
             for s, m in out_at.get(k, []):
                 empty(s, m, 0, HALF, False)
             add_reward(k, 0)
-            if k >= 1:
-                quant_q(k - 1)
-            for p in quant_at.get(k, []):
-                quant_v(p)
+            for s, g, lo, hi in quant_q_at.get(k, []):
+                quant_q(s, g, lo, hi)
+            for s in quant_at.get(k, []):
+                quant_v(s, 0, HALF)
             add_reward(k, 1)
             for s, t, on_vector in widen_at.get(k, []):
                 widen(s, t, on_vector)
-            for p, half in inter_at.get(k, []):
-                interleave(p, half)
+            for s in inter_at.get(k, []):
+                interleave(s, 0, HALF)
 
         tags = [("acc", 2), ("acc", 2), ("nxt", 3), ("nxt", 3)]
         for m in range(4):
             second_matmul(7, m, 0, QUARTER, tags[m][0], tags[m][1])
             empty(7, m, 0, QUARTER, m % 2 == 1)
-        quant_q(STEPS - 1)
+        quant_q(7, 1, QUARTER, HALF)
         tags = [("nxt", 3), ("turned", 3), ("turned", 3), ("turned", 3)]
         for m in range(4):
             second_matmul(7, m, QUARTER, HALF, tags[m][0], tags[m][1])

@@ -295,7 +295,7 @@ def tile_multi_world_bellman_backup_s14_kernel(
             quant_q_at.setdefault(k + 1, []).append((7, k % 2, lo, lo + QUARTER))
         for s in range(7):
             for m in range(4):
-                out_at.setdefault(min(4 * s + 5 + m, STEPS - 1), []).append((s, m))
+                out_at.setdefault(min(4 * s + 5 + m, STEPS), []).append((s, m))
 
         for t in (0, 1):
             widen(0, t, False, 0, QUARTER)
@@ -322,12 +322,13 @@ def tile_multi_world_bellman_backup_s14_kernel(
                 load_world(3)
             if k + 1 < STEPS:
                 first_matmul(k + 1)
+            if k + 1 < STEPS:
                 discount(k + 1)
-            for s, m in out_at.get(k, []):
-                second_matmul(s, m, 0, HALF, "acc", 2)
+            for s, m in out_at.get(k - 1, []):
+                empty(s, m, 0, HALF, False)
             transposes(k)
             for s, m in out_at.get(k, []):
-                empty(s, m, 0, HALF, False)
+                second_matmul(s, m, 0, HALF, "acc", 2)
             add_reward(k, 0)
             for s, g, lo, hi in quant_q_at.get(k, []):
                 quant_q(s, g, lo, hi)
@@ -339,13 +340,17 @@ def tile_multi_world_bellman_backup_s14_kernel(
             for s in inter_at.get(k, []):
                 interleave(s, 0, HALF)
 
-        tags = [("acc", 2), ("acc", 2), ("nxt", 3), ("nxt", 3)]
+        for s, m in out_at[STEPS - 1]:
+            empty(s, m, 0, HALF, False)
+        for s, m in out_at[STEPS]:
+            second_matmul(s, m, 0, HALF, "acc", 2)
+            empty(s, m, 0, HALF, False)
+        tags = [("nxt", 3), ("nxt", 3), ("nxt", 3), ("acc", 2)]
         for m in range(4):
             second_matmul(7, m, 0, QUARTER, tags[m][0], tags[m][1])
-            empty(7, m, 0, QUARTER, m % 2 == 1)
+            empty(7, m, 0, QUARTER, False)
         quant_q(7, 1, QUARTER, HALF)
-        tags = [("nxt", 3), ("turned", 3), ("turned", 3), ("turned", 3)]
+        tags = [("turned", 3), ("turned", 3), ("turned", 3), ("acc", 2)]
         for m in range(4):
             second_matmul(7, m, QUARTER, HALF, tags[m][0], tags[m][1])
-        for m in range(4):
-            empty(7, m, QUARTER, HALF, m % 2 == 1)
+            empty(7, m, QUARTER, HALF, m != 2)

from contextlib import ExitStack

import concourse.mybir as mybir
from concourse.masks import make_identity

E, S, L, T = 4, 512, 1024, 1024

FLOPS = 2 * E * (L * S * T + S * L * T)

F32 = mybir.dt.float32
BF16 = mybir.dt.bfloat16
I32 = mybir.dt.int32
U32 = mybir.dt.uint32
U8 = mybir.dt.uint8
FP8 = mybir.dt.float8_e4m3fn
FP8X4 = mybir.dt.float8_e4m3fn_x4
FP4X4 = mybir.dt.float4_e2m1fn_x4
COPY = mybir.ActivationFunctionType.Copy
MULT = mybir.AluOpType.mult
ADD = mybir.AluOpType.add

P = 128
PACK = 4
HALF = 512
QUARTER = 256
G = L // 512
STEPS = 32
V_PLANES = (0,)
RUN = 4


def tile_multi_world_bellman_backup_s14_kernel(
    tc, values_bytes, values_scale, trans_words, trans_scales, gamma, reward, pol_words, pol_scales, out
):
    nc = tc.nc
    with ExitStack() as ctx:
        keep = ctx.enter_context(tc.tile_pool(name="keep", bufs=1))
        work = ctx.enter_context(tc.tile_pool(name="work", bufs=2))
        psum = ctx.enter_context(tc.psum_pool(name="psum", bufs=2))
        ctx.enter_context(tc.manual_schedule())

        vscale = keep.tile([P, PACK], F32, name="vscale")
        nc.sync.dma_start(out=vscale[:], in_=values_scale.rearrange("o (p t) u -> p (o t u)", t=PACK))

        vbytes = {}

        def load_values(e, lo, hi):
            vb = keep.tile([P, PACK, hi - lo], U8, name="vb_%d_%d" % (e, lo))
            src = values_bytes[e].rearrange("(p t) n -> p t n", t=PACK)
            nc.sync.dma_start(out=vb[:], in_=src[:, :, lo:hi])
            vbytes[(e, lo, hi)] = vb

        def values_view(e, t, lo, hi):
            for key, vb in vbytes.items():
                if key[0] == e and key[1] <= lo and hi <= key[2]:
                    return vb[:, t, lo - key[1] : hi - key[1]].bitcast(FP8)
            raise AssertionError("no tile of values")

        tw = []

        def load_trans(e):
            w = keep.tile([P, 2 * L], U8, name="tw_%d" % e, align_bytes=64)
            nc.sync.dma_start(out=w[:], in_=trans_words[e])
            tw.append(w)

        pw = []

        def load_pol(e):
            w = keep.tile([P, G, 2 * S], U8, name="pw_%d" % e, align_bytes=64)
            nc.sync.dma_start(out=w[:], in_=pol_words[G * e : G * e + G].rearrange("g p n -> p g n"))
            pw.append(w)

        rew = {}

        def load_reward(e, g, lo, hi):
            r = keep.tile([P, PACK, hi - lo], BF16, name="rew_%d_%d_%d" % (e, g, lo))
            src = reward[e].rearrange("(g p t) n -> g p t n", p=P, t=PACK)[g]
            nc.sync.dma_start(out=r[:], in_=src[:, :, lo:hi])
            rew[(e, g, lo, hi)] = r

        def reward_view(e, g, lo, hi):
            for key, r in rew.items():
                if key[0] == e and key[1] == g and key[2] <= lo and hi <= key[3]:
                    return r[:, :, lo - key[2] : hi - key[2]]
            raise AssertionError("no tile of reward")

        ident = keep.tile([P, P], F32, name="ident")
        tsc = keep.tile([P, E, L], U8, name="tsc", align_bytes=64)
        psc = keep.tile([P, E * G, S], U8, name="psc", align_bytes=64)
        gam_rows = keep.tile([P, P], BF16, name="gam_rows")
        gam_f32 = keep.tile([P, P], F32, name="gam_f32")
        gcol = keep.tile([P, 32], F32, name="gcol")
        nc.vector.memset(tsc[:].rearrange("p e n -> p (e n)").bitcast(I32), 0)
        nc.gpsimd.memset(gam_rows[:], 0.0)
        make_identity(nc, ident[:])
        nc.vector.memset(psc[:].rearrange("p e n -> p (e n)").bitcast(I32), 0)

        load_values(0, 0, QUARTER)
        nc.sync.dma_start(out=gam_rows[0:32, :], in_=gamma.rearrange("e (j p) -> (e j) p", p=P))
        for q in range(4):
            nc.sync.dma_start(
                out=tsc[32 * q : 32 * q + 4].bitcast(I32),
                in_=trans_scales[:, 4 * q : 4 * q + 4, :].rearrange("g q n -> q g n").bitcast(I32),
            )
        load_trans(0)
        load_reward(0, 0, 0, QUARTER)
        load_reward(0, 1, 0, QUARTER)
        load_values(0, QUARTER, HALF)
        load_values(0, HALF, T)
        load_values(1, 0, T)
        load_reward(0, 0, QUARTER, HALF)
        load_reward(0, 1, QUARTER, HALF)
        for q in range(4):
            nc.sync.dma_start(
                out=psc[32 * q : 32 * q + 4].bitcast(I32),
                in_=pol_scales[:, 4 * q : 4 * q + 4, :].rearrange("g q n -> q g n").bitcast(I32),
            )
        load_pol(0)
        load_reward(0, 0, HALF, T)
        load_reward(0, 1, HALF, T)

        def load_world(e):
            if e > 1:
                load_values(e, 0, T)
            load_trans(e)
            load_reward(e, 0, 0, T)
            load_reward(e, 1, 0, T)
            load_pol(e)

        load_world(1)

        wide = {}

        def widen(s, t, on_vector, lo=0, hi=HALF):
            e, h = divmod(s, 2)
            if s not in wide:
                w = work.tile([P, PACK, HALF], BF16, name="wide", align_bytes=64)
                wide[s] = w
            src = values_view(e, t, HALF * h + lo, HALF * h + hi)
            dst = wide[s][:, t, lo:hi]
            if on_vector:
                nc.vector.tensor_scalar(out=dst, in0=src, scalar1=vscale[:, t : t + 1], scalar2=None, op0=MULT)
            else:
                nc.scalar.activation(out=dst, in_=src, func=COPY, scale=vscale[:, t : t + 1])

        inter = {}

        def interleave(s, lo, hi):
            x = work.tile([P, hi - lo, PACK], BF16, name="inter", align_bytes=64)
            inter[(s, lo)] = x
            src = wide[s][:, :, lo:hi]
            nc.vector.tensor_copy(
                out=x[:].rearrange("p (c i) t -> p c t i", i=RUN),
                in_=src.rearrange("p t (c i) -> p c t i", i=RUN),
            )

        vcodes = {}

        def quant_v(s, lo, hi):
            c = work.tile([P, hi - lo], U32, name="vcodes", align_bytes=64, bufs=3)
            sc = work.tile([P, hi - lo], U8, name="vcodes_sc", align_bytes=64, bufs=3)
            nc.vector.quantize_mx(
                out=c[:].bitcast(FP8X4), scales=sc[:], in_=inter[(s, lo)][:].rearrange("p n t -> p (n t)")
            )
            for a in range(lo, hi, QUARTER):
                vcodes[2 * s + a // QUARTER] = (c, sc, a - lo)

        nxt = {}

        def first_matmul(k):
            p, g = divmod(k, 2)
            e = k // 8
            c, sc, base = vcodes[p]
            for j in range(2):
                b = psum.tile([P, 512], F32, name="nxt", bufs=3)
                cols = slice(base + 128 * j, base + 128 * j + 128)
                nc.tensor.matmul_mx(
                    out=b[:],
                    lhsT=c[:, cols].bitcast(FP8X4),
                    lhsT_scale=sc[:, cols],
                    rhs=tw[e][:, 1024 * g : 1024 * g + 1024].bitcast(FP4X4),
                    rhs_scale=tsc[:, e, 512 * g : 512 * g + 512],
                    start=True,
                    stop=True,
                )
                nxt[(k, j)] = b

        disc = {}

        def discount(k):
            p = k // 2
            for j in range(2):
                jt = 2 * p + j
                d = work.tile([P, PACK, P], F32, name="disc", bufs=6)
                nc.scalar.activation(
                    out=d[:],
                    in_=nxt[(k, j)][:].rearrange("p (m t) -> p t m", t=PACK),
                    func=COPY,
                    scale=gcol[:, jt : jt + 1],
                )
                disc[(k, j)] = d

        turned = {}

        def transposes(k):
            for j in range(2):
                b = psum.tile([P, PACK, P], F32, name="turned", bufs=3)
                for t in range(PACK):
                    nc.tensor.transpose(b[:, t, :], disc[(k, j)][:, t, :], ident[:])
                turned[(k, j)] = b

        backed = {}

        def add_reward(k, j):
            p, g = divmod(k, 2)
            e, jt0 = p // 4, 2 * (p % 4)
            s, jp = divmod(p, 2)
            if j == 0 and jp == 0:
                q = work.tile([P, HALF, PACK], BF16, name="backed_%d" % g, align_bytes=64, bufs=2)
                backed[(s, g)] = q
            lo = 128 * (jt0 + j)
            at = QUARTER * jp + 128 * j
            nc.vector.tensor_tensor(
                out=backed[(s, g)][:, at : at + 128, :].rearrange("p (c i) t -> p c t i", i=RUN),
                in0=turned[(k, j)][:].rearrange("p t (c i) -> p c t i", i=RUN),
                in1=reward_view(e, g, lo, lo + 128).rearrange("p t (c i) -> p c t i", i=RUN),
                op=ADD,
            )

        qcodes = {}

        def quant_q(s, g, lo, hi):
            if lo == 0:
                c = work.tile([P, HALF], U32, name="qcodes_%d" % g, align_bytes=64)
                sc = work.tile([P, HALF], U8, name="qcodes_sc_%d" % g, align_bytes=64)
                qcodes[(s, g)] = (c, sc)
            c, sc = qcodes[(s, g)]
            nc.vector.quantize_mx(
                out=c[:, lo:hi].bitcast(FP8X4),
                scales=sc[:, lo:hi],
                in_=backed[(s, g)][:, lo:hi, :].rearrange("p n t -> p (n t)"),
            )

        accs = {}

        def second_matmul(s, m, lo, hi, tag, bufs):
            e = s // 2
            b = psum.tile([P, hi - lo], F32, name=tag, bufs=bufs)
            n = HALF if hi - lo == HALF else P
            for a in range(lo, hi, n):
                for g in range(G):
                    c, sc = qcodes[(s, g)]
                    nc.tensor.matmul_mx(
                        out=b[:, a - lo : a - lo + n],
                        lhsT=pw[e][:, g, 256 * m : 256 * m + 256].bitcast(FP4X4),
                        lhsT_scale=psc[:, G * e + g, 128 * m : 128 * m + 128],
                        rhs=c[:, a : a + n].bitcast(FP8X4),
                        rhs_scale=sc[:, a : a + n],
                        start=(g == 0),
                        stop=(g == G - 1),
                    )
            accs[(s, m, lo)] = b

        res = {}

        def empty(s, m, lo, hi, on_vector):
            if lo == 0:
                r = work.tile([P, HALF], F32, name="res", bufs=8)
                res[(s, m)] = r
            r = res[(s, m)]
            if on_vector:
                nc.vector.tensor_copy(out=r[:, lo:hi], in_=accs[(s, m, lo)][:])
            else:
                nc.scalar.copy(out=r[:, lo:hi], in_=accs[(s, m, lo)][:])
            if hi == HALF:
                e, h = divmod(s, 2)
                nc.sync.dma_start(out=out[e, 128 * m : 128 * m + 128, HALF * h : HALF * h + HALF], in_=r[:])

        widen_at, inter_at, quant_at, quant_q_at, out_at = {}, {}, {}, {}, {}
        for s in range(2, 8):
            on_s = [t for t in range(PACK) if t not in V_PLANES]
            for i, t in enumerate(on_s):
                widen_at.setdefault(4 * s - 7 + i, []).append((s, t, False))
            for t in V_PLANES:
                widen_at.setdefault(4 * s - 6, []).append((s, t, True))
        widen_at[0] = [(1, 2, False), (1, 3, False)]
        for s in range(1, 8):
            inter_at.setdefault(max(4 * s - 4, 1), []).append(s)
            quant_at.setdefault(max(4 * s - 3, 2), []).append(s)
        for s in range(7):
            for g in range(G):
                quant_q_at.setdefault(4 * s + 3 + g, []).append((s, g, 0, HALF))
        for k in range(28, STEPS - 1):
            lo = QUARTER * ((k - 28) // 2)
            quant_q_at.setdefault(k + 1, []).append((7, k % 2, lo, lo + QUARTER))
        for s in range(7):
            for m in range(4):
                out_at.setdefault(min(4 * s + 5 + m, STEPS), []).append((s, m))

        for t in (0, 1):
            widen(0, t, False, 0, QUARTER)
            widen(0, t + 2, True, 0, QUARTER)
        nc.vector.tensor_copy(out=gam_f32[:], in_=gam_rows[:])
        interleave(0, 0, QUARTER)
        quant_v(0, 0, QUARTER)
        turned_gamma = psum.tile([P, P], F32, name="acc", bufs=2)
        nc.tensor.transpose(turned_gamma[:], gam_f32[:], ident[:])
        nc.scalar.copy(out=gcol[:], in_=turned_gamma[:, 0:32])
        first_matmul(0)
        discount(0)
        for t in range(PACK):
            widen(0, t, True, QUARTER, HALF)
        interleave(0, QUARTER, HALF)
        widen(1, 0, True)
        quant_v(0, QUARTER, HALF)
        widen(1, 1, True)

        for k in range(STEPS):
            if k == 4:
                load_world(2)
            if k == 12:
                load_world(3)
            if k + 1 < STEPS:
                first_matmul(k + 1)
            if k + 1 < STEPS:
                discount(k + 1)
            for s, m in out_at.get(k - 1, []):
                empty(s, m, 0, HALF, False)
            transposes(k)
            for s, m in out_at.get(k, []):
                second_matmul(s, m, 0, HALF, "acc", 2)
            add_reward(k, 0)
            for s, g, lo, hi in quant_q_at.get(k, []):
                quant_q(s, g, lo, hi)
            for s in quant_at.get(k, []):
                quant_v(s, 0, HALF)
            add_reward(k, 1)
            for s, t, on_vector in widen_at.get(k, []):
                widen(s, t, on_vector)
            for s in inter_at.get(k, []):
                interleave(s, 0, HALF)

        for s, m in out_at[STEPS - 1]:
            empty(s, m, 0, HALF, False)
        for s, m in out_at[STEPS]:
            second_matmul(s, m, 0, HALF, "acc", 2)
            empty(s, m, 0, HALF, False)
        tags = [("nxt", 3), ("nxt", 3), ("nxt", 3), ("acc", 2)]
        for m in range(4):
            second_matmul(7, m, 0, QUARTER, tags[m][0], tags[m][1])
            empty(7, m, 0, QUARTER, False)
        quant_q(7, 1, QUARTER, HALF)
        tags = [("turned", 3), ("turned", 3), ("turned", 3), ("acc", 2)]
        for m in range(4):
            second_matmul(7, m, QUARTER, HALF, tags[m][0], tags[m][1])
            empty(7, m, QUARTER, HALF, m != 2)
